import numpy as np
import ml_dtypes


def mxq(x, axis, fmt="e4m3"):
    dtype, down = {"e4m3": (ml_dtypes.float8_e4m3fn, 7), "e5m2": (ml_dtypes.float8_e5m2, 14)}[fmt]
    v = np.moveaxis(np.asarray(x, np.float32).astype(ml_dtypes.bfloat16).astype(np.float64), axis, -1)
    blocks = v.reshape(v.shape[:-1] + (-1, 32))
    amax = np.abs(blocks).max(-1, keepdims=True)
    byte = np.maximum(np.where(amax > 0, np.frexp(amax)[1] - 1 + 127, 0) - down, 1)
    scale = np.exp2(byte - 127.0)
    codes = (blocks / scale).astype(np.float32).astype(dtype).astype(np.float64)
    return np.moveaxis((codes * scale).reshape(v.shape), -1, axis)


WIDE = False


def mx_kscale(k):
    if not WIDE:
        return np.ones(k)
    levels = np.array([10, -10, 5, -5, 0])
    if k % 512:
        return np.exp2(np.random.permutation(np.resize(levels, k // 32))).repeat(32)
    a = np.empty((k // 512, 16))
    for p in range(k // 512):
        a[p, :8] = np.random.permutation(np.resize(levels, 8))
        for g in range(8):
            far = levels[np.abs(levels - a[p, g]) >= 10]
            a[p, g + 8] = far[np.random.randint(len(far))]
    return np.exp2(a.ravel()).repeat(32)


def f64(x):
    return np.asarray(x).astype(np.float64)


def striped(idx):
    return np.tile(np.asarray(idx).reshape(-1, 16).T, (8, 1)).astype(np.uint16)


def unstriped(offs):
    return offs[:16].T.reshape(-1).astype(np.int64)


def striped8(idx):
    return np.asarray(idx).reshape(8, -1, 16).transpose(0, 2, 1).reshape(128, -1).astype(np.uint16)


def unstriped8(offs):
    return offs.reshape(8, 16, -1).transpose(0, 2, 1).reshape(8, -1).astype(np.int64)


def pick8(x, idx, run):
    r = np.arange(len(x))
    return x[r[:, None], idx[r % (8 * run) // run]]


E2M1 = np.array([0.0, 0.5, 1.0, 1.5, 2.0, 3.0, 4.0, 6.0, -0.0, -0.5, -1.0, -1.5, -2.0, -3.0, -4.0, -6.0])


def pack_weight(w, fmt):
    k, n = w.shape
    w = f64(np.asarray(w, np.float32).astype(ml_dtypes.bfloat16)).reshape(k // 32, 32, n)
    amax = np.abs(w).max(1)
    if fmt == "e4m3":
        byte = np.frexp(amax)[1] - 1 + 127 - 7
    else:
        mant, ex = np.frexp(amax / 6.0)
        byte = np.where(mant > 0.5, ex, ex - 1) + 127
    byte = np.clip(np.where(amax > 0, byte, 1), 1, 254)
    scaled = (w * np.exp2(127.0 - byte)[:, None, :]).reshape(k, n).astype(np.float32)
    by_word = np.ascontiguousarray(scaled.reshape(k // 512, 128, 4, n).transpose(0, 1, 3, 2))
    if fmt == "e4m3":
        words = by_word.astype(ml_dtypes.float8_e4m3fn).view(np.uint8)
    else:
        c = by_word.astype(ml_dtypes.float4_e2m1fn).view(np.uint8) & 0xF
        words = (c[..., 0::2] | (c[..., 1::2] << 4)).reshape(k // 512, 128, 2 * n)
    return np.ascontiguousarray(words), np.ascontiguousarray(byte.astype(np.uint8).reshape(k // 512, 16, n))


def unpack_weight(words, scales, fmt):
    g, _, n = scales.shape
    words = np.ascontiguousarray(words).reshape(g, 128, n, -1)
    if fmt == "e4m3":
        vals = words.view(ml_dtypes.float8_e4m3fn).astype(np.float64)
    else:
        nib = np.empty((g, 128, n, 4), np.uint8)
        nib[..., 0::2] = words & 0xF
        nib[..., 1::2] = words >> 4
        vals = E2M1[nib]
    vals = vals * np.repeat(np.exp2(scales.astype(np.float64) - 127.0), 8, axis=1)[..., None]
    return vals.transpose(0, 1, 3, 2).reshape(g * 512, n)


K, J, R, T, Z, M, C, D, N, S = 512, 384, 512, 1024, 512, 1024, 512, 1024, 256, 1024


def setup_inputs():
    n = np.random.standard_normal
    idx = np.random.permutation(T)[:J]
    idx2 = np.random.permutation(M)[:J]
    idx3 = np.stack([np.random.permutation(C)[:J] for _ in range(8)])
    idx4 = np.stack([np.random.permutation(D)[:C] for _ in range(8)])
    idx5 = np.random.permutation(S)[:N]
    fk = mx_kscale(K)
    fr = mx_kscale(R)
    fz = mx_kscale(Z)
    xtp = pack_weight(n((K, T)) * fk[:, None], "e2m1")
    wp = pack_weight(n((K, R)) * 1 / np.sqrt(K) / fk[:, None] * fr, "e4m3")
    xop = pack_weight(n((Z, M)) / fz[:, None], "e4m3")
    w2p = pack_weight(n((Z, R)) * 1 / np.sqrt(Z) * fz[:, None] * fr, "e2m1")
    vsp = pack_weight(n((R, S)) * 1 / np.sqrt(R) / fr[:, None], "e2m1")
    return {
        "xt_words": xtp[0],
        "xt_scales": xtp[1],
        "w_words": wp[0],
        "w_scales": wp[1],
        "xo_words": xop[0],
        "xo_scales": xop[1],
        "w2_words": w2p[0],
        "w2_scales": w2p[1],
        "tl": (np.random.randint(1, 9, (R, D)).astype(np.float64)).astype(np.float32),
        "sl": ((np.random.randint(4, 13, (R, 1)) / 64.0) * fr[:, None]).astype(np.float32),
        "vs_words": vsp[0],
        "vs_scales": vsp[1],
        "offs": striped(idx),
        "offs2": striped(idx2),
        "offs3": striped8(idx3),
        "offs4": striped8(idx4),
        "offs5": striped(idx5),
    }


def reference(xt_words, xt_scales, w_words, w_scales, xo_words, xo_scales, w2_words, w2_scales, tl, sl, vs_words, vs_scales, offs, offs2, offs3, offs4, offs5):
    idx = unstriped(offs)
    idx2 = unstriped(offs2)
    idx3 = unstriped8(offs3)
    idx4 = unstriped8(offs4)
    idx5 = unstriped(offs5)
    xtu = unpack_weight(xt_words, xt_scales, "e2m1")
    wu = unpack_weight(w_words, w_scales, "e4m3")
    xou = unpack_weight(xo_words, xo_scales, "e4m3")
    w2u = unpack_weight(w2_words, w2_scales, "e2m1")
    vsu = unpack_weight(vs_words, vs_scales, "e2m1")
    xtidxg = xtu[:, idx]
    xoidx2g = xou[:, idx2]
    a = wu.T @ xtidxg + w2u.T @ xoidx2g
    pw = np.zeros((R, C))
    pw[np.arange(R)[:, None], idx3[np.arange(R) % 512 // 64]] = a
    hid = np.maximum(np.abs(pw) - pick8(f64(tl), idx4, 64) * f64(sl), 0.0)
    vsidx5g = vsu[:, idx5]
    hidq = mxq(hid, 0, "e4m3")
    y = vsidx5g.T @ hidq
    return y

@@ -1,0 +1,191 @@
+from contextlib import ExitStack
+
+import concourse.mybir as mybir
+
+K, J, R, T, Z, M, C, D, N, S = 512, 384, 512, 1024, 512, 1024, 512, 1024, 256, 1024
+FLOPS = 2 * K * R * J + 2 * Z * R * J + 2 * R * N * C
+
+F32 = mybir.dt.float32
+BF16 = mybir.dt.bfloat16
+I32 = mybir.dt.int32
+U32 = mybir.dt.uint32
+U16 = mybir.dt.uint16
+U8 = mybir.dt.uint8
+FP8X4 = mybir.dt.float8_e4m3fn_x4
+FP4X4 = mybir.dt.float4_e2m1fn_x4
+ALU = mybir.AluOpType
+COPY = mybir.ActivationFunctionType.Copy
+
+P = 128
+PACK = 4
+QUADS = 4
+LIST = 16
+PIECES = ((0, 128), (128, 256))
+HALF = C // 2
+
+
+def tile_picked_tokens_plain_bank_shrunk_store_plain_kernel(
+    tc, xt_words, xt_scales, w_words, w_scales, xo_words, xo_scales, w2_words, w2_scales,
+    tl, sl, vs_words, vs_scales, offs, offs2, offs3, offs4, offs5, out,
+):
+    nc = tc.nc
+    with ExitStack() as ctx:
+        held = ctx.enter_context(tc.tile_pool(name="held", bufs=1))
+        psum = ctx.enter_context(tc.psum_pool(name="psum", bufs=1))
+
+        def sb(name, shape, dtype, tag=None):
+            return held.tile(shape, dtype, name=name, tag=tag or name, align_bytes=64)
+
+        def words32(dram):
+            return dram[0].rearrange("p n t -> p (n t)").bitcast(I32)
+
+        def by_quadrant(dram):
+            return dram[0].bitcast(I32).rearrange("(q r) n -> r q n", r=PACK)
+
+        xt_stage = sb("xt_stage", [PACK, QUADS, T // 4], I32)
+        xo_stage = sb("xo_stage", [PACK, QUADS, M // 4], I32)
+        ww_stage = sb("ww_stage", [PACK, QUADS, 2 * R // 4], I32)
+        xt_plane = sb("xt_plane", [P, T], U8)
+        xo_plane = sb("xo_plane", [P, M], U8)
+        ww_plane = sb("ww_plane", [P, 2 * R], U8)
+        vs_plane = sb("vs_plane", [P, S], U8)
+        tok_list = sb("tok_list", [P, J // LIST], U16)
+        note_list = sb("note_list", [P, J // LIST], U16)
+        board_list = sb("board_list", [P, J // LIST], U16)
+        level_list = sb("level_list", [P, C // LIST], U16)
+        store_list = sb("store_list", [P, N // LIST], U16)
+        xt_table = sb("xt_table", [P, T], U16)
+        xo_table = sb("xo_table", [P, M], U32)
+        vs_table = sb("vs_table", [P, S], U16)
+        w_raw = sb("w_raw", [P, R], U32)
+        w2_raw = sb("w2_raw", [P, R], U16)
+        step = sb("step", [P, PACK], F32)
+        levels = [sb("levels%d" % t, [P, D], F32) for t in range(PACK)]
+        boards = [sb("board%d" % t, [P, C], F32) for t in range(PACK)]
+
+        for plane in (xt_plane, xo_plane, ww_plane, vs_plane):
+            nc.vector.memset(plane[:].bitcast(I32), 0)
+        for t in range(PACK):
+            nc.gpsimd.memset(boards[t][:], 0.0)
+
+        tl_rows = tl.rearrange("(p t) d -> p t d", t=PACK)
+        nc.sync.dma_start(ww_stage[:, :, 0:R // 4], by_quadrant(w_scales))
+        nc.sync.dma_start(ww_stage[:, :, R // 4:], by_quadrant(w2_scales))
+        nc.sync.dma_start(xt_stage[:], by_quadrant(xt_scales))
+        nc.sync.dma_start(xo_stage[:], by_quadrant(xo_scales))
+        nc.sync.dma_start(w2_raw[:].bitcast(I32), w2_words[0].bitcast(I32))
+        nc.sync.dma_start(w_raw[:].bitcast(I32), words32(w_words))
+        nc.sync.dma_start(xt_table[:].bitcast(I32), xt_words[0].bitcast(I32))
+        nc.sync.dma_start(xo_table[:].bitcast(I32), words32(xo_words))
+        nc.sync.dma_start(tok_list[:], offs)
+        nc.sync.dma_start(note_list[:], offs2)
+        nc.sync.dma_start(level_list[:], offs4)
+        nc.sync.dma_start(step[:], sl.rearrange("(p t) o -> p (t o)", t=PACK))
+        nc.sync.dma_start(board_list[:], offs3)
+        for t in range(PACK):
+            nc.sync.dma_start(levels[t][:], tl_rows[:, t, :])
+        nc.sync.dma_start(store_list[:], offs5)
+        nc.sync.dma_start(vs_table[:].bitcast(I32), vs_words[0].bitcast(I32))
+        for q in range(QUADS):
+            nc.sync.dma_start(vs_plane[32 * q:32 * q + PACK, :].bitcast(I32), vs_scales[0][PACK * q:PACK * (q + 1), :].bitcast(I32))
+
+        for q in range(QUADS):
+            for stage, plane in ((ww_stage, ww_plane), (xo_stage, xo_plane), (xt_stage, xt_plane)):
+                nc.vector.tensor_copy(plane[32 * q:32 * q + PACK, :].bitcast(I32), stage[:, q, :])
+
+        ww_dealt = sb("ww_dealt", [P, 2 * R], U8)
+        nc.vector.tensor_copy(
+            ww_dealt[:].rearrange("p (a t m) -> p a t m", a=2, t=PACK),
+            ww_plane[:].rearrange("p (a m t) -> p a t m", a=2, t=PACK),
+        )
+        w_dealt = sb("w_dealt", [P, R], U32)
+        w2_dealt = sb("w2_dealt", [P, R], U16)
+        nc.scalar.copy(w2_dealt[:].rearrange("p (t m) -> p t m", t=PACK), w2_raw[:].rearrange("p (m t) -> p t m", t=PACK))
+        nc.scalar.copy(w_dealt[:].rearrange("p (t m) -> p t m", t=PACK), w_raw[:].rearrange("p (m t) -> p t m", t=PACK))
+
+        def fetch_levels(cut, t, h):
+            lo = h * HALF
+            nc.scalar.activation(
+                out=cut[:, t % 2, lo:lo + HALF],
+                in_=levels[t][:].indirect(level_list[:, lo // LIST:(lo + HALF) // LIST]),
+                func=COPY, scale=step[:, t:t + 1],
+            )
+
+        cut_early = sb("cut_early", [P, 2, C], F32)
+        for t in range(2):
+            for h in range(2):
+                fetch_levels(cut_early, t, h)
+
+        xt_got = sb("xt_got", [P, J], U16)
+        xo_got = sb("xo_got", [P, J], U32)
+        xts_got = sb("xts_got", [P, J], U8)
+        xos_got = sb("xos_got", [P, J], U8)
+        for j0, n in PIECES:
+            tok = tok_list[:, j0 // LIST:(j0 + n) // LIST]
+            note = note_list[:, j0 // LIST:(j0 + n) // LIST]
+            cols = slice(j0, j0 + n)
+            nc.vector.tensor_copy(xts_got[:, cols], xt_plane[:].indirect(tok))
+            nc.vector.tensor_copy(xt_got[:, cols], xt_table[:].indirect(tok))
+            nc.vector.tensor_copy(xos_got[:, cols], xo_plane[:].indirect(note))
+            nc.vector.tensor_copy(xo_got[:, cols], xo_table[:].indirect(note))
+            per_bank = 512 // n
+            hidden = sb("hidden%d" % j0, [P, PACK, n], F32, tag="levels0" if j0 == 0 else "late")
+            for b in range(PACK // per_bank):
+                acc = psum.tile([P, per_bank, n], F32, name="acc%d_%d" % (j0, b))
+                for i in range(per_bank):
+                    t = b * per_bank + i
+                    rows = slice(t * P, (t + 1) * P)
+                    nc.tensor.matmul_mx(
+                        out=acc[:, i, :], lhsT=w_dealt[:, rows].bitcast(FP8X4), lhsT_scale=ww_dealt[:, rows],
+                        rhs=xt_got[:, cols].bitcast(FP4X4), rhs_scale=xts_got[:, cols], start=True, stop=False,
+                    )
+                    nc.tensor.matmul_mx(
+                        out=acc[:, i, :], lhsT=w2_dealt[:, rows].bitcast(FP4X4), lhsT_scale=ww_dealt[:, R + t * P:R + (t + 1) * P],
+                        rhs=xo_got[:, cols].bitcast(FP8X4), rhs_scale=xos_got[:, cols], start=False, stop=True,
+                    )
+                nc.vector.tensor_copy(hidden[:, b * per_bank:(b + 1) * per_bank, :], acc[:])
+            for t in range(PACK):
+                nc.scalar.activation(
+                    out=boards[t][:].indirect(board_list[:, j0 // LIST:(j0 + n) // LIST]), in_=hidden[:, t, :], func=COPY,
+                )
+
+        vs_got = sb("vs_got", [P, N], U16)
+        vss_got = sb("vss_got", [P, N], U8)
+        nc.vector.tensor_copy(vs_got[:], vs_table[:].indirect(store_list[:]))
+        nc.vector.tensor_copy(vss_got[:], vs_plane[:].indirect(store_list[:]))
+
+        size = [sb("size%d" % t, [P, C], F32) for t in range(PACK)]
+        for t in range(PACK):
+            nc.vector.scalar_tensor_tensor(size[t][:], boards[t][:], -1.0, boards[t][:], ALU.mult, ALU.max)
+
+        cut_late = sb("cut_late", [P, 2, C], F32, tag="late")
+        for h in range(2):
+            cols = slice(h * HALF, (h + 1) * HALF)
+            over = sb("over%d" % h, [P, PACK, HALF], F32)
+            for t in range(PACK):
+                cut = cut_early if t < 2 else cut_late
+                if t >= 2:
+                    fetch_levels(cut_late, t, h)
+                nc.vector.tensor_tensor(over[:, t, :], size[t][:, cols], cut[:, t % 2, cols], ALU.subtract)
+            hid = sb("hid%d" % h, [P, HALF * PACK], BF16)
+            nc.vector.tensor_scalar(
+                hid[:].rearrange("p (c i t) -> p c t i", i=4, t=PACK),
+                over[:].rearrange("p t (c i) -> p c t i", i=4),
+                0.0, None, ALU.max,
+            )
+            codes = sb("codes%d" % h, [P, HALF], U32)
+            scales = sb("scales%d" % h, [P, HALF], U8)
+            nc.vector.quantize_mx(out=codes[:].bitcast(FP8X4), scales=scales[:], in_=hid[:])
+            for b in range(N // P):
+                rows = slice(b * P, (b + 1) * P)
+                res = psum.tile([P, HALF], F32, name="res%d_%d" % (h, b))
+                nc.tensor.matmul_mx(
+                    out=res[:], lhsT=vs_got[:, rows].bitcast(FP4X4), lhsT_scale=vss_got[:, rows],
+                    rhs=codes[:].bitcast(FP8X4), rhs_scale=scales[:], start=True, stop=True,
+                )
+                done = sb("done%d_%d" % (h, b), [P, HALF], F32)
+                if b == 0:
+                    nc.vector.tensor_copy(done[:], res[:])
+                else:
+                    nc.scalar.copy(done[:], res[:])
+                nc.sync.dma_start(out[rows, cols], done[:])

@@ -15,12 +15,14 @@ FP8X4 = mybir.dt.float8_e4m3fn_x4
 FP4X4 = mybir.dt.float4_e2m1fn_x4
 ALU = mybir.AluOpType
 COPY = mybir.ActivationFunctionType.Copy
+RELU = mybir.ActivationFunctionType.Relu
 
 P = 128
 PACK = 4
 QUADS = 4
 LIST = 16
-PIECES = ((0, 128), (128, 256))
+PIECES = ((0, 256), (256, 128))
+LAST = PACK - 1
 HALF = C // 2
 
 
@@ -71,108 +73,101 @@ def tile_picked_tokens_plain_bank_shrunk_store_plain_kernel(
         tl_rows = tl.rearrange("(p t) d -> p t d", t=PACK)
         nc.sync.dma_start(ww_stage[:, :, 0:R // 4], by_quadrant(w_scales))
         nc.sync.dma_start(ww_stage[:, :, R // 4:], by_quadrant(w2_scales))
-        nc.sync.dma_start(xt_stage[:], by_quadrant(xt_scales))
         nc.sync.dma_start(xo_stage[:], by_quadrant(xo_scales))
+        nc.sync.dma_start(xt_stage[:], by_quadrant(xt_scales))
         nc.sync.dma_start(w2_raw[:].bitcast(I32), w2_words[0].bitcast(I32))
-        nc.sync.dma_start(w_raw[:].bitcast(I32), words32(w_words))
-        nc.sync.dma_start(xt_table[:].bitcast(I32), xt_words[0].bitcast(I32))
-        nc.sync.dma_start(xo_table[:].bitcast(I32), words32(xo_words))
-        nc.sync.dma_start(tok_list[:], offs)
-        nc.sync.dma_start(note_list[:], offs2)
         nc.sync.dma_start(level_list[:], offs4)
         nc.sync.dma_start(step[:], sl.rearrange("(p t) o -> p (t o)", t=PACK))
-        nc.sync.dma_start(board_list[:], offs3)
-        for t in range(PACK):
-            nc.sync.dma_start(levels[t][:], tl_rows[:, t, :])
+        nc.sync.dma_start(levels[0][:], tl_rows[:, 0, :])
+        nc.sync.dma_start(note_list[:], offs2)
+        nc.sync.dma_start(tok_list[:], offs)
+        nc.sync.dma_start(xo_table[:].bitcast(I32), words32(xo_words))
+        nc.sync.dma_start(xt_table[:].bitcast(I32), xt_words[0].bitcast(I32))
+        nc.sync.dma_start(w_raw[:].bitcast(I32), words32(w_words))
+        nc.sync.dma_start(levels[1][:], tl_rows[:, 1, :])
+        nc.sync.dma_start(levels[2][:], tl_rows[:, 2, :])
         nc.sync.dma_start(store_list[:], offs5)
         nc.sync.dma_start(vs_table[:].bitcast(I32), vs_words[0].bitcast(I32))
         for q in range(QUADS):
             nc.sync.dma_start(vs_plane[32 * q:32 * q + PACK, :].bitcast(I32), vs_scales[0][PACK * q:PACK * (q + 1), :].bitcast(I32))
+        nc.sync.dma_start(board_list[:], offs3)
+        nc.sync.dma_start(levels[3][:], tl_rows[:, 3, :])
 
-        for q in range(QUADS):
-            for stage, plane in ((ww_stage, ww_plane), (xo_stage, xo_plane), (xt_stage, xt_plane)):
+        for stage, plane in ((ww_stage, ww_plane), (xo_stage, xo_plane), (xt_stage, xt_plane)):
+            for q in range(QUADS):
                 nc.vector.tensor_copy(plane[32 * q:32 * q + PACK, :].bitcast(I32), stage[:, q, :])
 
         ww_dealt = sb("ww_dealt", [P, 2 * R], U8)
-        nc.vector.tensor_copy(
+        nc.gpsimd.tensor_copy(
             ww_dealt[:].rearrange("p (a t m) -> p a t m", a=2, t=PACK),
             ww_plane[:].rearrange("p (a m t) -> p a t m", a=2, t=PACK),
         )
         w_dealt = sb("w_dealt", [P, R], U32)
         w2_dealt = sb("w2_dealt", [P, R], U16)
         nc.scalar.copy(w2_dealt[:].rearrange("p (t m) -> p t m", t=PACK), w2_raw[:].rearrange("p (m t) -> p t m", t=PACK))
-        nc.scalar.copy(w_dealt[:].rearrange("p (t m) -> p t m", t=PACK), w_raw[:].rearrange("p (m t) -> p t m", t=PACK))
 
-        def fetch_levels(cut, t, h):
-            lo = h * HALF
+        def fetch_levels(dst, t, lo, n):
             nc.scalar.activation(
-                out=cut[:, t % 2, lo:lo + HALF],
-                in_=levels[t][:].indirect(level_list[:, lo // LIST:(lo + HALF) // LIST]),
+                out=dst[:, lo:lo + n], in_=levels[t][:].indirect(level_list[:, lo // LIST:(lo + n) // LIST]),
                 func=COPY, scale=step[:, t:t + 1],
             )
 
-        cut_early = sb("cut_early", [P, 2, C], F32)
-        for t in range(2):
-            for h in range(2):
-                fetch_levels(cut_early, t, h)
+        cut = [sb("cut%d" % t, [P, C], F32) for t in range(LAST)]
+        fetch_levels(cut[0], 0, 0, C)
+        nc.scalar.copy(w_dealt[:].rearrange("p (t m) -> p t m", t=PACK), w_raw[:].rearrange("p (m t) -> p t m", t=PACK))
+        for t in range(1, LAST):
+            fetch_levels(cut[t], t, 0, C)
 
         xt_got = sb("xt_got", [P, J], U16)
         xo_got = sb("xo_got", [P, J], U32)
         xts_got = sb("xts_got", [P, J], U8)
         xos_got = sb("xos_got", [P, J], U8)
-        for j0, n in PIECES:
-            tok = tok_list[:, j0 // LIST:(j0 + n) // LIST]
-            note = note_list[:, j0 // LIST:(j0 + n) // LIST]
-            cols = slice(j0, j0 + n)
-            nc.vector.tensor_copy(xts_got[:, cols], xt_plane[:].indirect(tok))
-            nc.vector.tensor_copy(xt_got[:, cols], xt_table[:].indirect(tok))
-            nc.vector.tensor_copy(xos_got[:, cols], xo_plane[:].indirect(note))
-            nc.vector.tensor_copy(xo_got[:, cols], xo_table[:].indirect(note))
-            per_bank = 512 // n
-            hidden = sb("hidden%d" % j0, [P, PACK, n], F32, tag="levels0" if j0 == 0 else "late")
-            for b in range(PACK // per_bank):
-                acc = psum.tile([P, per_bank, n], F32, name="acc%d_%d" % (j0, b))
-                for i in range(per_bank):
-                    t = b * per_bank + i
-                    rows = slice(t * P, (t + 1) * P)
-                    nc.tensor.matmul_mx(
-                        out=acc[:, i, :], lhsT=w_dealt[:, rows].bitcast(FP8X4), lhsT_scale=ww_dealt[:, rows],
-                        rhs=xt_got[:, cols].bitcast(FP4X4), rhs_scale=xts_got[:, cols], start=True, stop=False,
-                    )
-                    nc.tensor.matmul_mx(
-                        out=acc[:, i, :], lhsT=w2_dealt[:, rows].bitcast(FP4X4), lhsT_scale=ww_dealt[:, R + t * P:R + (t + 1) * P],
-                        rhs=xo_got[:, cols].bitcast(FP8X4), rhs_scale=xos_got[:, cols], start=False, stop=True,
-                    )
-                nc.vector.tensor_copy(hidden[:, b * per_bank:(b + 1) * per_bank, :], acc[:])
-            for t in range(PACK):
-                nc.scalar.activation(
-                    out=boards[t][:].indirect(board_list[:, j0 // LIST:(j0 + n) // LIST]), in_=hidden[:, t, :], func=COPY,
+        nc.vector.tensor_copy(xos_got[:], xo_plane[:].indirect(note_list[:]))
+        nc.vector.tensor_copy(xts_got[:], xt_plane[:].indirect(tok_list[:]))
+        nc.vector.tensor_copy(xo_got[:], xo_table[:].indirect(note_list[:]))
+        nc.vector.tensor_copy(xt_got[:], xt_table[:].indirect(tok_list[:]))
+        for t in range(PACK):
+            rows = slice(t * P, (t + 1) * P)
+            acc = psum.tile([P, J], F32, name="acc%d" % t)
+            for j0, n in PIECES:
+                nc.tensor.matmul_mx(
+                    out=acc[:, j0:j0 + n], lhsT=w2_dealt[:, rows].bitcast(FP4X4), lhsT_scale=ww_dealt[:, R + t * P:R + (t + 1) * P],
+                    rhs=xo_got[:, j0:j0 + n].bitcast(FP8X4), rhs_scale=xos_got[:, j0:j0 + n], start=(j0 == 0), stop=False,
                 )
+            for j0, n in PIECES:
+                nc.tensor.matmul_mx(
+                    out=acc[:, j0:j0 + n], lhsT=w_dealt[:, rows].bitcast(FP8X4), lhsT_scale=ww_dealt[:, rows],
+                    rhs=xt_got[:, j0:j0 + n].bitcast(FP4X4), rhs_scale=xts_got[:, j0:j0 + n], start=False, stop=(j0 + n == J),
+                )
+            hidden = sb("hidden%d" % t, [P, J], F32)
+            minus = sb("minus%d" % t, [P, J], F32)
+            nc.vector.tensor_scalar(minus[:], acc[:], -1.0, None, ALU.mult)
+            nc.vector.tensor_tensor(hidden[:], acc[:], minus[:], ALU.max)
+            nc.scalar.activation(out=boards[t][:].indirect(board_list[:]), in_=hidden[:], func=COPY)
 
         vs_got = sb("vs_got", [P, N], U16)
         vss_got = sb("vss_got", [P, N], U8)
         nc.vector.tensor_copy(vs_got[:], vs_table[:].indirect(store_list[:]))
         nc.vector.tensor_copy(vss_got[:], vs_plane[:].indirect(store_list[:]))
 
-        size = [sb("size%d" % t, [P, C], F32) for t in range(PACK)]
-        for t in range(PACK):
-            nc.vector.scalar_tensor_tensor(size[t][:], boards[t][:], -1.0, boards[t][:], ALU.mult, ALU.max)
+        over = sb("over", [P, PACK, C], F32)
+        for t in range(LAST):
+            nc.vector.tensor_tensor(over[:, t, :], boards[t][:], cut[t][:], ALU.subtract)
 
-        cut_late = sb("cut_late", [P, 2, C], F32, tag="late")
+        cut_last = sb("cut_last", [P, C], F32, tag="hidden%d" % LAST)
         for h in range(2):
             cols = slice(h * HALF, (h + 1) * HALF)
-            over = sb("over%d" % h, [P, PACK, HALF], F32)
-            for t in range(PACK):
-                cut = cut_early if t < 2 else cut_late
-                if t >= 2:
-                    fetch_levels(cut_late, t, h)
-                nc.vector.tensor_tensor(over[:, t, :], size[t][:, cols], cut[:, t % 2, cols], ALU.subtract)
+            fetch_levels(cut_last, LAST, h * HALF, HALF)
+            nc.vector.tensor_tensor(over[:, LAST, cols], boards[LAST][:, cols], cut_last[:, cols], ALU.subtract)
+        for h in range(2):
+            cols = slice(h * HALF, (h + 1) * HALF)
             hid = sb("hid%d" % h, [P, HALF * PACK], BF16)
-            nc.vector.tensor_scalar(
-                hid[:].rearrange("p (c i t) -> p c t i", i=4, t=PACK),
-                over[:].rearrange("p t (c i) -> p c t i", i=4),
-                0.0, None, ALU.max,
-            )
+            on_vector = HALF if h == 0 else HALF // 2
+            woven = hid[:].rearrange("p (c i t) -> p c t i", i=4, t=PACK)
+            apart = over[:, :, cols].rearrange("p t (c i) -> p c t i", i=4)
+            nc.vector.tensor_scalar(woven[:, :on_vector // 4], apart[:, :on_vector // 4], 0.0, None, ALU.max)
+            if on_vector < HALF:
+                nc.scalar.activation(out=woven[:, on_vector // 4:], in_=apart[:, on_vector // 4:], func=RELU)
             codes = sb("codes%d" % h, [P, HALF], U32)
             scales = sb("scales%d" % h, [P, HALF], U8)
             nc.vector.quantize_mx(out=codes[:].bitcast(FP8X4), scales=scales[:], in_=hid[:])
@@ -184,7 +179,7 @@ def tile_picked_tokens_plain_bank_shrunk_store_plain_kernel(
                     rhs=codes[:].bitcast(FP8X4), rhs_scale=scales[:], start=True, stop=True,
                 )
                 done = sb("done%d_%d" % (h, b), [P, HALF], F32)
-                if b == 0:
+                if b == 0 and h == 1:
                     nc.vector.tensor_copy(done[:], res[:])
                 else:
                     nc.scalar.copy(done[:], res[:])

@@ -47,6 +47,7 @@ def tile_picked_tokens_plain_bank_shrunk_store_plain_kernel(
         xt_stage = sb("xt_stage", [PACK, QUADS, T // 4], I32)
         xo_stage = sb("xo_stage", [PACK, QUADS, M // 4], I32)
         ww_stage = sb("ww_stage", [PACK, QUADS, 2 * R // 4], I32)
+        vs_stage = sb("vs_stage", [PACK, QUADS, S // 4], I32)
         xt_plane = sb("xt_plane", [P, T], U8)
         xo_plane = sb("xo_plane", [P, M], U8)
         ww_plane = sb("ww_plane", [P, 2 * R], U8)
@@ -65,16 +66,16 @@ def tile_picked_tokens_plain_bank_shrunk_store_plain_kernel(
         levels = [sb("levels%d" % t, [P, D], F32) for t in range(PACK)]
         boards = [sb("board%d" % t, [P, C], F32) for t in range(PACK)]
 
-        for plane in (xt_plane, xo_plane, ww_plane, vs_plane):
+        for plane in (xo_plane, xt_plane, ww_plane, vs_plane):
             nc.vector.memset(plane[:].bitcast(I32), 0)
         for t in range(PACK):
-            nc.gpsimd.memset(boards[t][:], 0.0)
+            (nc.vector if t < 2 else nc.gpsimd).memset(boards[t][:], 0.0)
 
         tl_rows = tl.rearrange("(p t) d -> p t d", t=PACK)
-        nc.sync.dma_start(ww_stage[:, :, 0:R // 4], by_quadrant(w_scales))
-        nc.sync.dma_start(ww_stage[:, :, R // 4:], by_quadrant(w2_scales))
         nc.sync.dma_start(xo_stage[:], by_quadrant(xo_scales))
         nc.sync.dma_start(xt_stage[:], by_quadrant(xt_scales))
+        nc.sync.dma_start(ww_stage[:, :, 0:R // 4], by_quadrant(w_scales))
+        nc.sync.dma_start(ww_stage[:, :, R // 4:], by_quadrant(w2_scales))
         nc.sync.dma_start(w2_raw[:].bitcast(I32), w2_words[0].bitcast(I32))
         nc.sync.dma_start(level_list[:], offs4)
         nc.sync.dma_start(step[:], sl.rearrange("(p t) o -> p (t o)", t=PACK))
@@ -86,16 +87,19 @@ def tile_picked_tokens_plain_bank_shrunk_store_plain_kernel(
         nc.sync.dma_start(w_raw[:].bitcast(I32), words32(w_words))
         nc.sync.dma_start(levels[1][:], tl_rows[:, 1, :])
         nc.sync.dma_start(levels[2][:], tl_rows[:, 2, :])
+        nc.sync.dma_start(vs_stage[:], by_quadrant(vs_scales))
         nc.sync.dma_start(store_list[:], offs5)
-        nc.sync.dma_start(vs_table[:].bitcast(I32), vs_words[0].bitcast(I32))
-        for q in range(QUADS):
-            nc.sync.dma_start(vs_plane[32 * q:32 * q + PACK, :].bitcast(I32), vs_scales[0][PACK * q:PACK * (q + 1), :].bitcast(I32))
         nc.sync.dma_start(board_list[:], offs3)
+        nc.sync.dma_start(vs_table[:].bitcast(I32), vs_words[0].bitcast(I32))
         nc.sync.dma_start(levels[3][:], tl_rows[:, 3, :])
 
-        for stage, plane in ((ww_stage, ww_plane), (xo_stage, xo_plane), (xt_stage, xt_plane)):
+        def spread(stage, plane):
             for q in range(QUADS):
                 nc.vector.tensor_copy(plane[32 * q:32 * q + PACK, :].bitcast(I32), stage[:, q, :])
+
+        spread(xo_stage, xo_plane)
+        spread(xt_stage, xt_plane)
+        spread(ww_stage, ww_plane)
 
         ww_dealt = sb("ww_dealt", [P, 2 * R], U8)
         nc.gpsimd.tensor_copy(
@@ -104,7 +108,7 @@ def tile_picked_tokens_plain_bank_shrunk_store_plain_kernel(
         )
         w_dealt = sb("w_dealt", [P, R], U32)
         w2_dealt = sb("w2_dealt", [P, R], U16)
-        nc.scalar.copy(w2_dealt[:].rearrange("p (t m) -> p t m", t=PACK), w2_raw[:].rearrange("p (m t) -> p t m", t=PACK))
+        nc.scalar.copy(w2_dealt[:].rearrange("p (t m) -> p m t", t=PACK), w2_raw[:].rearrange("p (m t) -> p m t", t=PACK))
 
         def fetch_levels(dst, t, lo, n):
             nc.scalar.activation(
@@ -114,7 +118,7 @@ def tile_picked_tokens_plain_bank_shrunk_store_plain_kernel(
 
         cut = [sb("cut%d" % t, [P, C], F32) for t in range(LAST)]
         fetch_levels(cut[0], 0, 0, C)
-        nc.scalar.copy(w_dealt[:].rearrange("p (t m) -> p t m", t=PACK), w_raw[:].rearrange("p (m t) -> p t m", t=PACK))
+        nc.scalar.copy(w_dealt[:].rearrange("p (t m) -> p m t", t=PACK), w_raw[:].rearrange("p (m t) -> p m t", t=PACK))
         for t in range(1, LAST):
             fetch_levels(cut[t], t, 0, C)
 
@@ -140,11 +144,15 @@ def tile_picked_tokens_plain_bank_shrunk_store_plain_kernel(
                     rhs=xt_got[:, j0:j0 + n].bitcast(FP4X4), rhs_scale=xts_got[:, j0:j0 + n], start=False, stop=(j0 + n == J),
                 )
             hidden = sb("hidden%d" % t, [P, J], F32)
-            minus = sb("minus%d" % t, [P, J], F32)
-            nc.vector.tensor_scalar(minus[:], acc[:], -1.0, None, ALU.mult)
-            nc.vector.tensor_tensor(hidden[:], acc[:], minus[:], ALU.max)
+            if t < LAST:
+                nc.vector.tensor_copy(hidden[:], acc[:])
+            else:
+                minus = sb("minus%d" % t, [P, J], F32)
+                nc.vector.tensor_scalar(minus[:], acc[:], -1.0, None, ALU.mult)
+                nc.vector.tensor_tensor(hidden[:], acc[:], minus[:], ALU.max)
             nc.scalar.activation(out=boards[t][:].indirect(board_list[:]), in_=hidden[:], func=COPY)
 
+        spread(vs_stage, vs_plane)
         vs_got = sb("vs_got", [P, N], U16)
         vss_got = sb("vss_got", [P, N], U8)
         nc.vector.tensor_copy(vs_got[:], vs_table[:].indirect(store_list[:]))
@@ -152,7 +160,9 @@ def tile_picked_tokens_plain_bank_shrunk_store_plain_kernel(
 
         over = sb("over", [P, PACK, C], F32)
         for t in range(LAST):
-            nc.vector.tensor_tensor(over[:, t, :], boards[t][:], cut[t][:], ALU.subtract)
+            size = sb("size%d" % t, [P, C], F32, tag="minus%d" % LAST)
+            nc.vector.scalar_tensor_tensor(size[:], boards[t][:], -1.0, boards[t][:], ALU.mult, ALU.max)
+            nc.vector.tensor_tensor(over[:, t, :], size[:], cut[t][:], ALU.subtract)
 
         cut_last = sb("cut_last", [P, C], F32, tag="hidden%d" % LAST)
         for h in range(2):

@@ -51,7 +51,6 @@ def tile_picked_tokens_plain_bank_shrunk_store_plain_kernel(
         xt_plane = sb("xt_plane", [P, T], U8)
         xo_plane = sb("xo_plane", [P, M], U8)
         ww_plane = sb("ww_plane", [P, 2 * R], U8)
-        vs_plane = sb("vs_plane", [P, S], U8)
         tok_list = sb("tok_list", [P, J // LIST], U16)
         note_list = sb("note_list", [P, J // LIST], U16)
         board_list = sb("board_list", [P, J // LIST], U16)
@@ -66,7 +65,7 @@ def tile_picked_tokens_plain_bank_shrunk_store_plain_kernel(
         levels = [sb("levels%d" % t, [P, D], F32) for t in range(PACK)]
         boards = [sb("board%d" % t, [P, C], F32) for t in range(PACK)]
 
-        for plane in (xo_plane, xt_plane, ww_plane, vs_plane):
+        for plane in (xo_plane, xt_plane, ww_plane):
             nc.vector.memset(plane[:].bitcast(I32), 0)
         for t in range(PACK):
             (nc.vector if t < 2 else nc.gpsimd).memset(boards[t][:], 0.0)
@@ -76,13 +75,13 @@ def tile_picked_tokens_plain_bank_shrunk_store_plain_kernel(
         nc.sync.dma_start(xt_stage[:], by_quadrant(xt_scales))
         nc.sync.dma_start(ww_stage[:, :, 0:R // 4], by_quadrant(w_scales))
         nc.sync.dma_start(ww_stage[:, :, R // 4:], by_quadrant(w2_scales))
+        nc.sync.dma_start(note_list[:], offs2)
+        nc.sync.dma_start(tok_list[:], offs)
+        nc.sync.dma_start(levels[0][:], tl_rows[:, 0, :])
+        nc.sync.dma_start(xo_table[:].bitcast(I32), words32(xo_words))
         nc.sync.dma_start(w2_raw[:].bitcast(I32), w2_words[0].bitcast(I32))
         nc.sync.dma_start(level_list[:], offs4)
         nc.sync.dma_start(step[:], sl.rearrange("(p t) o -> p (t o)", t=PACK))
-        nc.sync.dma_start(levels[0][:], tl_rows[:, 0, :])
-        nc.sync.dma_start(note_list[:], offs2)
-        nc.sync.dma_start(tok_list[:], offs)
-        nc.sync.dma_start(xo_table[:].bitcast(I32), words32(xo_words))
         nc.sync.dma_start(xt_table[:].bitcast(I32), xt_words[0].bitcast(I32))
         nc.sync.dma_start(w_raw[:].bitcast(I32), words32(w_words))
         nc.sync.dma_start(levels[1][:], tl_rows[:, 1, :])
@@ -152,17 +151,18 @@ def tile_picked_tokens_plain_bank_shrunk_store_plain_kernel(
                 nc.vector.tensor_tensor(hidden[:], acc[:], minus[:], ALU.max)
             nc.scalar.activation(out=boards[t][:].indirect(board_list[:]), in_=hidden[:], func=COPY)
 
+        vs_plane = sb("vs_plane", [P, S], U8, tag="ww_dealt")
+        nc.vector.memset(vs_plane[:].bitcast(I32), 0)
         spread(vs_stage, vs_plane)
-        vs_got = sb("vs_got", [P, N], U16)
+        vs_got = sb("vs_got", [P, N], U16, tag="xt_got")
         vss_got = sb("vss_got", [P, N], U8)
         nc.vector.tensor_copy(vs_got[:], vs_table[:].indirect(store_list[:]))
         nc.vector.tensor_copy(vss_got[:], vs_plane[:].indirect(store_list[:]))
 
-        over = sb("over", [P, PACK, C], F32)
+        over = sb("over", [P, PACK, C], F32, tag="minus%d" % LAST)
         for t in range(LAST):
-            size = sb("size%d" % t, [P, C], F32, tag="minus%d" % LAST)
-            nc.vector.scalar_tensor_tensor(size[:], boards[t][:], -1.0, boards[t][:], ALU.mult, ALU.max)
-            nc.vector.tensor_tensor(over[:, t, :], size[:], cut[t][:], ALU.subtract)
+            nc.vector.scalar_tensor_tensor(over[:, LAST, :], boards[t][:], -1.0, boards[t][:], ALU.mult, ALU.max)
+            nc.vector.tensor_tensor(over[:, t, :], over[:, LAST, :], cut[t][:], ALU.subtract)
 
         cut_last = sb("cut_last", [P, C], F32, tag="hidden%d" % LAST)
         for h in range(2):

@@ -92,16 +92,16 @@ def tile_picked_tokens_plain_bank_shrunk_store_plain_kernel(
         nc.sync.dma_start(vs_table[:].bitcast(I32), vs_words[0].bitcast(I32))
         nc.sync.dma_start(levels[3][:], tl_rows[:, 3, :])
 
-        def spread(stage, plane):
-            for q in range(QUADS):
+        def spread(stage, plane, quads):
+            for q in quads:
                 nc.vector.tensor_copy(plane[32 * q:32 * q + PACK, :].bitcast(I32), stage[:, q, :])
 
-        spread(xo_stage, xo_plane)
-        spread(xt_stage, xt_plane)
-        spread(ww_stage, ww_plane)
+        spread(xo_stage, xo_plane, range(QUADS))
+        spread(xt_stage, xt_plane, reversed(range(QUADS)))
+        spread(ww_stage, ww_plane, range(QUADS))
 
         ww_dealt = sb("ww_dealt", [P, 2 * R], U8)
-        nc.gpsimd.tensor_copy(
+        nc.vector.tensor_copy(
             ww_dealt[:].rearrange("p (a t m) -> p a t m", a=2, t=PACK),
             ww_plane[:].rearrange("p (a m t) -> p a t m", a=2, t=PACK),
         )
@@ -128,7 +128,8 @@ def tile_picked_tokens_plain_bank_shrunk_store_plain_kernel(
         nc.vector.tensor_copy(xos_got[:], xo_plane[:].indirect(note_list[:]))
         nc.vector.tensor_copy(xts_got[:], xt_plane[:].indirect(tok_list[:]))
         nc.vector.tensor_copy(xo_got[:], xo_table[:].indirect(note_list[:]))
-        nc.vector.tensor_copy(xt_got[:], xt_table[:].indirect(tok_list[:]))
+        for j0, n in PIECES:
+            nc.vector.tensor_copy(xt_got[:, j0:j0 + n], xt_table[:].indirect(tok_list[:, j0 // LIST:(j0 + n) // LIST]))
         for t in range(PACK):
             rows = slice(t * P, (t + 1) * P)
             acc = psum.tile([P, J], F32, name="acc%d" % t)
@@ -153,7 +154,7 @@ def tile_picked_tokens_plain_bank_shrunk_store_plain_kernel(
 
         vs_plane = sb("vs_plane", [P, S], U8, tag="ww_dealt")
         nc.vector.memset(vs_plane[:].bitcast(I32), 0)
-        spread(vs_stage, vs_plane)
+        spread(vs_stage, vs_plane, range(QUADS))
         vs_got = sb("vs_got", [P, N], U16, tag="xt_got")
         vss_got = sb("vss_got", [P, N], U8)
         nc.vector.tensor_copy(vs_got[:], vs_table[:].indirect(store_list[:]))

from contextlib import ExitStack

import concourse.mybir as mybir

K, J, R, T, Z, M, C, D, N, S = 512, 384, 512, 1024, 512, 1024, 512, 1024, 256, 1024
FLOPS = 2 * K * R * J + 2 * Z * R * J + 2 * R * N * C

F32 = mybir.dt.float32
BF16 = mybir.dt.bfloat16
I32 = mybir.dt.int32
U32 = mybir.dt.uint32
U16 = mybir.dt.uint16
U8 = mybir.dt.uint8
FP8X4 = mybir.dt.float8_e4m3fn_x4
FP4X4 = mybir.dt.float4_e2m1fn_x4
ALU = mybir.AluOpType
COPY = mybir.ActivationFunctionType.Copy
RELU = mybir.ActivationFunctionType.Relu

P = 128
PACK = 4
QUADS = 4
LIST = 16
PIECES = ((0, 256), (256, 128))
LAST = PACK - 1
HALF = C // 2


def tile_picked_tokens_plain_bank_shrunk_store_plain_kernel(
    tc, xt_words, xt_scales, w_words, w_scales, xo_words, xo_scales, w2_words, w2_scales,
    tl, sl, vs_words, vs_scales, offs, offs2, offs3, offs4, offs5, out,
):
    nc = tc.nc
    with ExitStack() as ctx:
        held = ctx.enter_context(tc.tile_pool(name="held", bufs=1))
        psum = ctx.enter_context(tc.psum_pool(name="psum", bufs=1))

        def sb(name, shape, dtype, tag=None):
            return held.tile(shape, dtype, name=name, tag=tag or name, align_bytes=64)

        def words32(dram):
            return dram[0].rearrange("p n t -> p (n t)").bitcast(I32)

        def by_quadrant(dram):
            return dram[0].bitcast(I32).rearrange("(q r) n -> r q n", r=PACK)

        xt_stage = sb("xt_stage", [PACK, QUADS, T // 4], I32)
        xo_stage = sb("xo_stage", [PACK, QUADS, M // 4], I32)
        ww_stage = sb("ww_stage", [PACK, QUADS, 2 * R // 4], I32)
        vs_stage = sb("vs_stage", [PACK, QUADS, S // 4], I32)
        xt_plane = sb("xt_plane", [P, T], U8)
        xo_plane = sb("xo_plane", [P, M], U8)
        ww_plane = sb("ww_plane", [P, 2 * R], U8)
        tok_list = sb("tok_list", [P, J // LIST], U16)
        note_list = sb("note_list", [P, J // LIST], U16)
        board_list = sb("board_list", [P, J // LIST], U16)
        level_list = sb("level_list", [P, C // LIST], U16)
        store_list = sb("store_list", [P, N // LIST], U16)
        xt_table = sb("xt_table", [P, T], U16)
        xo_table = sb("xo_table", [P, M], U32)
        vs_table = sb("vs_table", [P, S], U16)
        w_raw = sb("w_raw", [P, R], U32)
        w2_raw = sb("w2_raw", [P, R], U16)
        step = sb("step", [P, PACK], F32)
        levels = [sb("levels%d" % t, [P, D], F32) for t in range(PACK)]
        boards = [sb("board%d" % t, [P, C], F32) for t in range(PACK)]

        for plane in (xo_plane, xt_plane, ww_plane):
            nc.vector.memset(plane[:].bitcast(I32), 0)
        for t in range(PACK):
            (nc.vector if t < 2 else nc.gpsimd).memset(boards[t][:], 0.0)

        tl_rows = tl.rearrange("(p t) d -> p t d", t=PACK)
        nc.sync.dma_start(xo_stage[:], by_quadrant(xo_scales))
        nc.sync.dma_start(xt_stage[:], by_quadrant(xt_scales))
        nc.sync.dma_start(ww_stage[:, :, 0:R // 4], by_quadrant(w_scales))
        nc.sync.dma_start(ww_stage[:, :, R // 4:], by_quadrant(w2_scales))
        nc.sync.dma_start(note_list[:], offs2)
        nc.sync.dma_start(tok_list[:], offs)
        nc.sync.dma_start(levels[0][:], tl_rows[:, 0, :])
        nc.sync.dma_start(xo_table[:].bitcast(I32), words32(xo_words))
        nc.sync.dma_start(w2_raw[:].bitcast(I32), w2_words[0].bitcast(I32))
        nc.sync.dma_start(level_list[:], offs4)
        nc.sync.dma_start(step[:], sl.rearrange("(p t) o -> p (t o)", t=PACK))
        nc.sync.dma_start(xt_table[:].bitcast(I32), xt_words[0].bitcast(I32))
        nc.sync.dma_start(w_raw[:].bitcast(I32), words32(w_words))
        nc.sync.dma_start(levels[1][:], tl_rows[:, 1, :])
        nc.sync.dma_start(levels[2][:], tl_rows[:, 2, :])
        nc.sync.dma_start(vs_stage[:], by_quadrant(vs_scales))
        nc.sync.dma_start(store_list[:], offs5)
        nc.sync.dma_start(board_list[:], offs3)
        nc.sync.dma_start(vs_table[:].bitcast(I32), vs_words[0].bitcast(I32))
        nc.sync.dma_start(levels[3][:], tl_rows[:, 3, :])

        def spread(stage, plane, quads):
            for q in quads:
                nc.vector.tensor_copy(plane[32 * q:32 * q + PACK, :].bitcast(I32), stage[:, q, :])

        spread(xo_stage, xo_plane, range(QUADS))
        spread(xt_stage, xt_plane, reversed(range(QUADS)))
        spread(ww_stage, ww_plane, range(QUADS))

        ww_dealt = sb("ww_dealt", [P, 2 * R], U8)
        nc.vector.tensor_copy(
            ww_dealt[:].rearrange("p (a t m) -> p a t m", a=2, t=PACK),
            ww_plane[:].rearrange("p (a m t) -> p a t m", a=2, t=PACK),
        )
        w_dealt = sb("w_dealt", [P, R], U32)
        w2_dealt = sb("w2_dealt", [P, R], U16)
        nc.scalar.copy(w2_dealt[:].rearrange("p (t m) -> p m t", t=PACK), w2_raw[:].rearrange("p (m t) -> p m t", t=PACK))

        def fetch_levels(dst, t, lo, n):
            nc.scalar.activation(
                out=dst[:, lo:lo + n], in_=levels[t][:].indirect(level_list[:, lo // LIST:(lo + n) // LIST]),
                func=COPY, scale=step[:, t:t + 1],
            )

        cut = [sb("cut%d" % t, [P, C], F32) for t in range(LAST)]
        fetch_levels(cut[0], 0, 0, C)
        nc.scalar.copy(w_dealt[:].rearrange("p (t m) -> p m t", t=PACK), w_raw[:].rearrange("p (m t) -> p m t", t=PACK))
        for t in range(1, LAST):
            fetch_levels(cut[t], t, 0, C)

        xt_got = sb("xt_got", [P, J], U16)
        xo_got = sb("xo_got", [P, J], U32)
        xts_got = sb("xts_got", [P, J], U8)
        xos_got = sb("xos_got", [P, J], U8)
        nc.vector.tensor_copy(xos_got[:], xo_plane[:].indirect(note_list[:]))
        nc.vector.tensor_copy(xts_got[:], xt_plane[:].indirect(tok_list[:]))
        nc.vector.tensor_copy(xo_got[:], xo_table[:].indirect(note_list[:]))
        for j0, n in PIECES:
            nc.vector.tensor_copy(xt_got[:, j0:j0 + n], xt_table[:].indirect(tok_list[:, j0 // LIST:(j0 + n) // LIST]))
        for t in range(PACK):
            rows = slice(t * P, (t + 1) * P)
            acc = psum.tile([P, J], F32, name="acc%d" % t)
            for j0, n in PIECES:
                nc.tensor.matmul_mx(
                    out=acc[:, j0:j0 + n], lhsT=w2_dealt[:, rows].bitcast(FP4X4), lhsT_scale=ww_dealt[:, R + t * P:R + (t + 1) * P],
                    rhs=xo_got[:, j0:j0 + n].bitcast(FP8X4), rhs_scale=xos_got[:, j0:j0 + n], start=(j0 == 0), stop=False,
                )
            for j0, n in PIECES:
                nc.tensor.matmul_mx(
                    out=acc[:, j0:j0 + n], lhsT=w_dealt[:, rows].bitcast(FP8X4), lhsT_scale=ww_dealt[:, rows],
                    rhs=xt_got[:, j0:j0 + n].bitcast(FP4X4), rhs_scale=xts_got[:, j0:j0 + n], start=False, stop=(j0 + n == J),
                )
            hidden = sb("hidden%d" % t, [P, J], F32)
            if t < LAST:
                nc.vector.tensor_copy(hidden[:], acc[:])
            else:
                minus = sb("minus%d" % t, [P, J], F32)
                nc.vector.tensor_scalar(minus[:], acc[:], -1.0, None, ALU.mult)
                nc.vector.tensor_tensor(hidden[:], acc[:], minus[:], ALU.max)
            nc.scalar.activation(out=boards[t][:].indirect(board_list[:]), in_=hidden[:], func=COPY)

        vs_plane = sb("vs_plane", [P, S], U8, tag="ww_dealt")
        nc.vector.memset(vs_plane[:].bitcast(I32), 0)
        spread(vs_stage, vs_plane, range(QUADS))
        vs_got = sb("vs_got", [P, N], U16, tag="xt_got")
        vss_got = sb("vss_got", [P, N], U8)
        nc.vector.tensor_copy(vs_got[:], vs_table[:].indirect(store_list[:]))
        nc.vector.tensor_copy(vss_got[:], vs_plane[:].indirect(store_list[:]))

        over = sb("over", [P, PACK, C], F32, tag="minus%d" % LAST)
        for t in range(LAST):
            nc.vector.scalar_tensor_tensor(over[:, LAST, :], boards[t][:], -1.0, boards[t][:], ALU.mult, ALU.max)
            nc.vector.tensor_tensor(over[:, t, :], over[:, LAST, :], cut[t][:], ALU.subtract)

        cut_last = sb("cut_last", [P, C], F32, tag="hidden%d" % LAST)
        for h in range(2):
            cols = slice(h * HALF, (h + 1) * HALF)
            fetch_levels(cut_last, LAST, h * HALF, HALF)
            nc.vector.tensor_tensor(over[:, LAST, cols], boards[LAST][:, cols], cut_last[:, cols], ALU.subtract)
        for h in range(2):
            cols = slice(h * HALF, (h + 1) * HALF)
            hid = sb("hid%d" % h, [P, HALF * PACK], BF16)
            on_vector = HALF if h == 0 else HALF // 2
            woven = hid[:].rearrange("p (c i t) -> p c t i", i=4, t=PACK)
            apart = over[:, :, cols].rearrange("p t (c i) -> p c t i", i=4)
            nc.vector.tensor_scalar(woven[:, :on_vector // 4], apart[:, :on_vector // 4], 0.0, None, ALU.max)
            if on_vector < HALF:
                nc.scalar.activation(out=woven[:, on_vector // 4:], in_=apart[:, on_vector // 4:], func=RELU)
            codes = sb("codes%d" % h, [P, HALF], U32)
            scales = sb("scales%d" % h, [P, HALF], U8)
            nc.vector.quantize_mx(out=codes[:].bitcast(FP8X4), scales=scales[:], in_=hid[:])
            for b in range(N // P):
                rows = slice(b * P, (b + 1) * P)
                res = psum.tile([P, HALF], F32, name="res%d_%d" % (h, b))
                nc.tensor.matmul_mx(
                    out=res[:], lhsT=vs_got[:, rows].bitcast(FP4X4), lhsT_scale=vss_got[:, rows],
                    rhs=codes[:].bitcast(FP8X4), rhs_scale=scales[:], start=True, stop=True,
                )
                done = sb("done%d_%d" % (h, b), [P, HALF], F32)
                if b == 0 and h == 1:
                    nc.vector.tensor_copy(done[:], res[:])
                else:
                    nc.scalar.copy(done[:], res[:])
                nc.sync.dma_start(out[rows, cols], done[:])
